import numpy as np
import ml_dtypes


def mxq(x, axis, fmt="e4m3"):
    dtype, down = {"e4m3": (ml_dtypes.float8_e4m3fn, 7), "e5m2": (ml_dtypes.float8_e5m2, 14)}[fmt]
    v = np.moveaxis(np.asarray(x, np.float32).astype(ml_dtypes.bfloat16).astype(np.float64), axis, -1)
    blocks = v.reshape(v.shape[:-1] + (-1, 32))
    amax = np.abs(blocks).max(-1, keepdims=True)
    byte = np.maximum(np.where(amax > 0, np.frexp(amax)[1] - 1 + 127, 0) - down, 1)
    scale = np.exp2(byte - 127.0)
    codes = (blocks / scale).astype(np.float32).astype(dtype).astype(np.float64)
    return np.moveaxis((codes * scale).reshape(v.shape), -1, axis)


WIDE = False


def mx_kscale(k, group=512):
    if not WIDE:
        return np.ones(k)
    levels = np.array([18, -18])
    if group != 512:
        return np.exp2(np.random.permutation(np.resize(levels, k // group))).repeat(group)
    if k % 512:
        return np.exp2(np.random.permutation(np.resize(levels, k // 32))).repeat(32)
    a = np.empty((k // 512, 16))
    for p in range(k // 512):
        a[p, :8] = np.random.permutation(np.resize(levels, 8))
        for g in range(8):
            far = levels[np.abs(levels - a[p, g]) >= 10]
            a[p, g + 8] = far[np.random.randint(len(far))]
    return np.exp2(a.ravel()).repeat(32)


def f64(x):
    return np.asarray(x).astype(np.float64)


def silu(v):
    return v / (1.0 + np.exp(-v))


def sigmoid(v):
    return 1.0 / (1.0 + np.exp(-v))


G, D, M, O, N = 4, 128, 128, 128, 512


def setup_inputs():
    n = np.random.standard_normal
    s_d = mx_kscale(D, 0)
    s_o = mx_kscale(O, 0)
    return {
        "x": (n((G, D, N)) * s_d[:, None]).astype(np.float32),
        "w1": (n((G, D, M)) / np.sqrt(D) / s_d[:, None]).astype(np.float32),
        "w2": (n((G, D, M)) / np.sqrt(D) / s_d[:, None]).astype(np.float32),
        "w3": (n((G, D, M)) / np.sqrt(D) / s_d[:, None]).astype(np.float32),
        "b3": (0.5 * n((G, M, 1))).astype(np.float32),
        "wo": (n((G, O, M)) / np.sqrt(O) / s_o[:, None]).astype(np.float32),
        "dy": (n((G, O, N)) * s_o[:, None]).astype(np.float32),
        "old": (0.3 * n((G, M, N))).astype(np.float32),
    }


def reference(x, w1, w2, w3, b3, wo, dy, old):
    w1q = mxq(f64(w1), 1, "e4m3")
    xq = mxq(f64(x), 1, "e4m3")
    z1 = w1q.transpose(0, 2, 1) @ xq
    w2q = mxq(f64(w2), 1, "e4m3")
    z2 = w2q.transpose(0, 2, 1) @ xq
    w3q = mxq(f64(w3), 1, "e4m3")
    z3 = w3q.transpose(0, 2, 1) @ xq
    e1 = np.tanh(z1)
    e2 = silu(z2)
    gt = sigmoid(z3 + f64(b3))
    woq = mxq(f64(wo), 1, "e4m3")
    dyq = mxq(f64(dy), 1, "e4m3")
    c0 = woq.transpose(0, 2, 1) @ dyq
    dgt = c0 * (e1 - e2)
    dz3 = dgt * gt * (1.0 - gt)
    y = dz3 + f64(old)
    return y

@@ -1,0 +1,198 @@
+from contextlib import ExitStack
+
+import concourse.mybir as mybir
+
+G, D, M, N = 4, 128, 128, 512
+FLOPS = 4 * 2 * G * D * M * N
+
+F32 = mybir.dt.float32
+BF16 = mybir.dt.bfloat16
+U32 = mybir.dt.uint32
+U8 = mybir.dt.uint8
+FP8X4 = mybir.dt.float8_e4m3fn_x4
+ACT = mybir.ActivationFunctionType
+ALU = mybir.AluOpType
+
+P = 128
+PACK = 4
+ROWS = D // PACK
+HALF = N // 2
+MM_N = 128
+RUN = 4
+
+
+def tile_rows_bmixture_kernel(tc, x, w1, w2, w3, b3, wo, dy, old, out):
+    nc = tc.nc
+    with ExitStack() as ctx:
+        sb = ctx.enter_context(tc.tile_pool(name="sb", bufs=1))
+        ps = ctx.enter_context(tc.psum_pool(name="ps", bufs=1))
+        ctx.enter_context(tc.manual_schedule())
+
+        def operand(name, width):
+            return {
+                "raw": sb.tile([P, PACK, width], F32, name=name + "_raw"),
+                "bf": sb.tile([P, width, PACK], BF16, name=name + "_bf", align_bytes=64),
+                "codes": sb.tile([P, width], U32, name=name + "_codes", align_bytes=64),
+                "scales": sb.tile([P, width], U8, name=name + "_scales", align_bytes=64),
+            }
+
+        def load(op, src, cols):
+            nc.sync.dma_start(out=op["raw"][:], in_=src.rearrange("g (p j) n -> (g p) j n", j=PACK)[:, :, cols])
+
+        def interleave(copy, op, cols=slice(None)):
+            copy(
+                out=op["bf"][:, cols, :].rearrange("p (c i) j -> p c j i", i=RUN),
+                in_=op["raw"][:, :, cols].rearrange("p j (c i) -> p c j i", i=RUN),
+            )
+
+        def quantize(op):
+            nc.vector.quantize_mx(
+                out=op["codes"][:].bitcast(FP8X4),
+                scales=op["scales"][:],
+                in_=op["bf"][:].rearrange("p n j -> p (n j)"),
+            )
+
+        def product(g, bank, at, w, a):
+            rows = slice(ROWS * g, ROWS * (g + 1))
+            for n0 in range(0, HALF, MM_N):
+                nc.tensor.matmul_mx(
+                    out=bank[:, at + n0 : at + n0 + MM_N],
+                    lhsT=w["codes"][rows, :].bitcast(FP8X4),
+                    lhsT_scale=w["scales"][rows, :],
+                    rhs=a["codes"][rows, n0 : n0 + MM_N].bitcast(FP8X4),
+                    rhs_scale=a["scales"][rows, n0 : n0 + MM_N],
+                    start=True,
+                    stop=True,
+                )
+
+        groups = range(G)
+        halves = [slice(0, HALF), slice(HALF, N)]
+        w1q, w2q, w3q, woq = operand("w1", M), operand("w2", M), operand("w3", M), operand("wo", M)
+        xq = [operand("x0", HALF), operand("x1", HALF)]
+        dyq = [operand("dy0", HALF), operand("dy1", HALF)]
+        bank_a = [ps.tile([P, N], F32, name="bank_a%d" % g) for g in groups]
+        bank_b = [ps.tile([P, N], F32, name="bank_b%d" % g) for g in groups]
+
+        def half_tiles(name):
+            return [sb.tile([P, G, HALF], F32, name="%s%d" % (name, h)) for h in range(2)]
+
+        e1, e2, th, sq = half_tiles("e1"), half_tiles("e2"), half_tiles("th"), half_tiles("sq")
+        diff, dgt, dz3, old_sb, res = half_tiles("diff"), half_tiles("dgt"), half_tiles("dz3"), half_tiles("old"), half_tiles("res")
+        b_rows = sb.tile([P, G * ROWS], F32, align_bytes=64)
+        b_cols = sb.tile([P, G * ROWS], F32, align_bytes=64)
+        b_half = sb.tile([P, G], F32)
+
+        def silu_z2(h, g, bank, at):
+            nc.scalar.activation(out=e2[h][:, g, :], in_=bank[:, at : at + HALF], func=ACT.Silu)
+
+        def tanh_z1(h, g, bank, at):
+            nc.scalar.activation(out=e1[h][:, g, :], in_=bank[:, at : at + HALF], func=ACT.Tanh)
+
+        def tanh_z3(h, g, bank, at):
+            nc.scalar.activation(out=th[h][:, g, :], in_=bank[:, at : at + HALF], func=ACT.Tanh, bias=b_half[:, g : g + 1], scale=0.5)
+
+        def square(h, gs):
+            nc.scalar.activation(out=sq[h][:, gs, :], in_=th[h][:, gs, :], func=ACT.Square, scale=0.5)
+
+        def v_diff(h, gs):
+            nc.vector.tensor_tensor(out=diff[h][:, gs, :], in0=e2[h][:, gs, :], in1=e1[h][:, gs, :], op=ALU.subtract)
+
+        def v_dgt(h, g):
+            nc.vector.tensor_tensor(out=dgt[h][:, g, :], in0=bank_b[g][:, 0:HALF], in1=diff[h][:, g, :], op=ALU.mult)
+
+        def v_dz3(h, gs):
+            nc.vector.scalar_tensor_tensor(out=dz3[h][:, gs, :], in0=sq[h][:, gs, :], scalar=0.25, in1=dgt[h][:, gs, :], op0=ALU.subtract, op1=ALU.mult)
+
+        def v_res(h, gs):
+            nc.vector.tensor_tensor(out=res[h][:, gs, :], in0=dz3[h][:, gs, :], in1=old_sb[h][:, gs, :], op=ALU.add)
+
+        def store(h, gs):
+            nc.sync.dma_start(out=out.rearrange("g m n -> m g n")[:, gs, halves[h]], in_=res[h][:, gs, :])
+
+        everything = slice(0, G)
+        one = [slice(g, g + 1) for g in groups]
+        pairs = [slice(0, 2), slice(2, 4)]
+
+        nc.gpsimd.memset(b_rows[:], 0.0)
+        nc.scalar.dma_start(
+            out=b_rows[0:P:ROWS, :].rearrange("q (g i) -> q g i", g=G),
+            in_=b3.rearrange("g (q i) o -> q g (i o)", i=ROWS),
+        )
+        load(w2q, w2, slice(0, M))
+        load(xq[0], x, halves[0])
+        load(w1q, w1, slice(0, M))
+        load(w3q, w3, slice(0, M))
+        load(woq, wo, slice(0, M))
+        load(dyq[0], dy, halves[0])
+        load(xq[1], x, halves[1])
+        load(dyq[1], dy, halves[1])
+        for h in range(2):
+            nc.sync.dma_start(out=old_sb[h][:], in_=old.rearrange("g m n -> m g n")[:, :, halves[h]])
+
+        vcopy, scopy = nc.vector.tensor_copy, nc.scalar.copy
+        interleave(vcopy, w2q)
+        nc.vector.transpose(out=b_cols[:], in_=b_rows[:])
+        quantize(w2q)
+        nc.vector.tensor_scalar(out=b_half[:], in0=b_cols[:, 0 : G * ROWS : ROWS], scalar1=0.5, scalar2=None, op0=ALU.mult)
+        interleave(vcopy, xq[0])
+        interleave(vcopy, w1q)
+        quantize(xq[0])
+        for g in groups:
+            product(g, bank_a[g], 0, w2q, xq[0])
+        interleave(vcopy, w3q)
+        quantize(w1q)
+        for g in groups:
+            product(g, bank_b[g], 0, w1q, xq[0])
+        for g in groups:
+            silu_z2(0, g, bank_a[g], 0)
+        interleave(vcopy, woq)
+        quantize(w3q)
+        for g in groups:
+            product(g, bank_a[g], 0, w3q, xq[0])
+        for g in groups:
+            tanh_z1(0, g, bank_b[g], 0)
+        quantize(woq)
+        interleave(vcopy, dyq[0])
+        for g in groups:
+            tanh_z3(0, g, bank_a[g], 0)
+        quantize(dyq[0])
+        v_diff(0, pairs[0])
+        for g in groups:
+            product(g, bank_b[g], 0, woq, dyq[0])
+        interleave(vcopy, xq[1])
+        v_diff(0, pairs[1])
+        interleave(scopy, dyq[1])
+        quantize(xq[1])
+        v_dgt(0, 0)
+        for g in groups:
+            product(g, bank_a[g], 0, w2q, xq[1])
+            product(g, bank_a[g], HALF, w1q, xq[1])
+        for g in groups[1:]:
+            v_dgt(0, g)
+        quantize(dyq[1])
+        for g in groups:
+            product(g, bank_b[g], 0, woq, dyq[1])
+            product(g, bank_b[g], HALF, w3q, xq[1])
+        for gs in pairs:
+            square(0, gs)
+            v_dz3(0, gs)
+        for gs in pairs:
+            v_res(0, gs)
+            store(0, gs)
+
+        for step in range(G + 1):
+            if step < G:
+                silu_z2(1, step, bank_a[step], 0)
+            if step > 0:
+                square(1, one[step - 1])
+            if step < G:
+                tanh_z1(1, step, bank_a[step], HALF)
+                tanh_z3(1, step, bank_b[step], HALF)
+                v_diff(1, one[step])
+            if step > 0:
+                v_dz3(1, one[step - 1])
+            if step < G:
+                v_dgt(1, step)
+            if step > 0:
+                v_res(1, one[step - 1])
+                store(1, one[step - 1])

@@ -103,8 +103,8 @@ def tile_rows_bmixture_kernel(tc, x, w1, w2, w3, b3, wo, dy, old, out):
         def v_dz3(h, gs):
             nc.vector.scalar_tensor_tensor(out=dz3[h][:, gs, :], in0=sq[h][:, gs, :], scalar=0.25, in1=dgt[h][:, gs, :], op0=ALU.subtract, op1=ALU.mult)
 
-        def v_res(h, gs):
-            nc.vector.tensor_tensor(out=res[h][:, gs, :], in0=dz3[h][:, gs, :], in1=old_sb[h][:, gs, :], op=ALU.add)
+        def v_res(h, gs, engine=nc.vector):
+            engine.tensor_tensor(out=res[h][:, gs, :], in0=dz3[h][:, gs, :], in1=old_sb[h][:, gs, :], op=ALU.add)
 
         def store(h, gs):
             nc.sync.dma_start(out=out.rearrange("g m n -> m g n")[:, gs, halves[h]], in_=res[h][:, gs, :])
@@ -113,86 +113,96 @@ def tile_rows_bmixture_kernel(tc, x, w1, w2, w3, b3, wo, dy, old, out):
         one = [slice(g, g + 1) for g in groups]
         pairs = [slice(0, 2), slice(2, 4)]
 
-        nc.gpsimd.memset(b_rows[:], 0.0)
-        nc.scalar.dma_start(
+        warm_in = sb.tile([P, 1], F32)
+        warm_out = sb.tile([P, 1], F32)
+        nc.vector.memset(warm_in[:], 0.0)
+        nc.vector.memset(b_rows[:], 0.0)
+        nc.scalar.activation(out=warm_out[:], in_=warm_in[:], func=ACT.Silu)
+        load(xq[0], x, halves[0])
+        load(w2q, w2, slice(0, M))
+        load(w1q, w1, slice(0, M))
+        load(w3q, w3, slice(0, M))
+        nc.sync.dma_start(
             out=b_rows[0:P:ROWS, :].rearrange("q (g i) -> q g i", g=G),
             in_=b3.rearrange("g (q i) o -> q g (i o)", i=ROWS),
         )
-        load(w2q, w2, slice(0, M))
-        load(xq[0], x, halves[0])
-        load(w1q, w1, slice(0, M))
-        load(w3q, w3, slice(0, M))
-        load(woq, wo, slice(0, M))
         load(dyq[0], dy, halves[0])
+        load(woq, wo, slice(0, M))
         load(xq[1], x, halves[1])
         load(dyq[1], dy, halves[1])
         for h in range(2):
             nc.sync.dma_start(out=old_sb[h][:], in_=old.rearrange("g m n -> m g n")[:, :, halves[h]])
 
         vcopy, scopy = nc.vector.tensor_copy, nc.scalar.copy
+        lo, hi = [0, 1], [2, 3]
+        interleave(vcopy, xq[0], slice(0, 160))
+        interleave(scopy, xq[0], slice(160, HALF))
         interleave(vcopy, w2q)
-        nc.vector.transpose(out=b_cols[:], in_=b_rows[:])
-        quantize(w2q)
-        nc.vector.tensor_scalar(out=b_half[:], in0=b_cols[:, 0 : G * ROWS : ROWS], scalar1=0.5, scalar2=None, op0=ALU.mult)
-        interleave(vcopy, xq[0])
-        interleave(vcopy, w1q)
         quantize(xq[0])
+        interleave(scopy, w1q)
+        quantize(w2q)
         for g in groups:
             product(g, bank_a[g], 0, w2q, xq[0])
         interleave(vcopy, w3q)
         quantize(w1q)
         for g in groups:
             product(g, bank_b[g], 0, w1q, xq[0])
+        nc.vector.transpose(out=b_cols[:], in_=b_rows[:])
+        quantize(w3q)
+        nc.vector.tensor_scalar(out=b_half[:], in0=b_cols[:, 0 : G * ROWS : ROWS], scalar1=0.5, scalar2=None, op0=ALU.mult)
         for g in groups:
             silu_z2(0, g, bank_a[g], 0)
-        interleave(vcopy, woq)
-        quantize(w3q)
-        for g in groups:
             product(g, bank_a[g], 0, w3q, xq[0])
         for g in groups:
             tanh_z1(0, g, bank_b[g], 0)
-        quantize(woq)
         interleave(vcopy, dyq[0])
-        for g in groups:
-            tanh_z3(0, g, bank_a[g], 0)
+        interleave(vcopy, woq)
         quantize(dyq[0])
-        v_diff(0, pairs[0])
+        quantize(woq)
         for g in groups:
             product(g, bank_b[g], 0, woq, dyq[0])
-        interleave(vcopy, xq[1])
+        v_diff(0, pairs[0])
+        for g in lo:
+            tanh_z3(0, g, bank_a[g], 0)
+        interleave(scopy, xq[1], slice(192, HALF))
+        tanh_z3(0, 2, bank_a[2], 0)
+        square(0, pairs[0])
+        tanh_z3(0, 3, bank_a[3], 0)
+        interleave(vcopy, xq[1], slice(0, 192))
         v_diff(0, pairs[1])
-        interleave(scopy, dyq[1])
+        for g in lo:
+            v_dgt(0, g)
         quantize(xq[1])
-        v_dgt(0, 0)
         for g in groups:
             product(g, bank_a[g], 0, w2q, xq[1])
             product(g, bank_a[g], HALF, w1q, xq[1])
-        for g in groups[1:]:
+        interleave(scopy, dyq[1], slice(0, HALF))
+        square(0, pairs[1])
+        v_dz3(0, pairs[0])
+        for g in hi:
             v_dgt(0, g)
+        v_res(0, pairs[0])
+        store(0, pairs[0])
         quantize(dyq[1])
         for g in groups:
             product(g, bank_b[g], 0, woq, dyq[1])
             product(g, bank_b[g], HALF, w3q, xq[1])
-        for gs in pairs:
-            square(0, gs)
-            v_dz3(0, gs)
-        for gs in pairs:
-            v_res(0, gs)
-            store(0, gs)
-
-        for step in range(G + 1):
-            if step < G:
-                silu_z2(1, step, bank_a[step], 0)
-            if step > 0:
-                square(1, one[step - 1])
-            if step < G:
-                tanh_z1(1, step, bank_a[step], HALF)
-                tanh_z3(1, step, bank_b[step], HALF)
-                v_diff(1, one[step])
-            if step > 0:
-                v_dz3(1, one[step - 1])
-            if step < G:
-                v_dgt(1, step)
-            if step > 0:
-                v_res(1, one[step - 1])
-                store(1, one[step - 1])
+        for g in hi:
+            v_dz3(0, one[g])
+        for g in hi:
+            v_res(0, one[g])
+        store(0, pairs[1])
+        for pair in (lo, hi):
+            for g in pair:
+                silu_z2(1, g, bank_a[g], 0)
+                tanh_z1(1, g, bank_a[g], HALF)
+            for g in pair:
+                tanh_z3(1, g, bank_b[g], HALF)
+            for g in pair:
+                square(1, one[g])
+            for step in (v_diff, v_dgt, v_dz3):
+                for g in pair:
+                    step(1, g if step == v_dgt else one[g])
+            for g in pair:
+                v_res(1, one[g])
+                store(1, one[g])

@@ -52,18 +52,19 @@ def tile_rows_bmixture_kernel(tc, x, w1, w2, w3, b3, wo, dy, old, out):
                 in_=op["bf"][:].rearrange("p n j -> p (n j)"),
             )
 
-        def product(g, bank, at, w, a):
-            rows = slice(ROWS * g, ROWS * (g + 1))
+        def products(gs, banks, at, w, a):
             for n0 in range(0, HALF, MM_N):
-                nc.tensor.matmul_mx(
-                    out=bank[:, at + n0 : at + n0 + MM_N],
-                    lhsT=w["codes"][rows, :].bitcast(FP8X4),
-                    lhsT_scale=w["scales"][rows, :],
-                    rhs=a["codes"][rows, n0 : n0 + MM_N].bitcast(FP8X4),
-                    rhs_scale=a["scales"][rows, n0 : n0 + MM_N],
-                    start=True,
-                    stop=True,
-                )
+                for g in gs:
+                    rows = slice(ROWS * g, ROWS * (g + 1))
+                    nc.tensor.matmul_mx(
+                        out=banks[g][:, at + n0 : at + n0 + MM_N],
+                        lhsT=w["codes"][rows, :].bitcast(FP8X4),
+                        lhsT_scale=w["scales"][rows, :],
+                        rhs=a["codes"][rows, n0 : n0 + MM_N].bitcast(FP8X4),
+                        rhs_scale=a["scales"][rows, n0 : n0 + MM_N],
+                        start=True,
+                        stop=True,
+                    )
 
         groups = range(G)
         halves = [slice(0, HALF), slice(HALF, N)]
@@ -141,26 +142,23 @@ def tile_rows_bmixture_kernel(tc, x, w1, w2, w3, b3, wo, dy, old, out):
         quantize(xq[0])
         interleave(scopy, w1q)
         quantize(w2q)
-        for g in groups:
-            product(g, bank_a[g], 0, w2q, xq[0])
+        products(groups, bank_a, 0, w2q, xq[0])
         interleave(vcopy, w3q)
         quantize(w1q)
-        for g in groups:
-            product(g, bank_b[g], 0, w1q, xq[0])
+        products(groups, bank_b, 0, w1q, xq[0])
         nc.vector.transpose(out=b_cols[:], in_=b_rows[:])
         quantize(w3q)
         nc.vector.tensor_scalar(out=b_half[:], in0=b_cols[:, 0 : G * ROWS : ROWS], scalar1=0.5, scalar2=None, op0=ALU.mult)
         for g in groups:
             silu_z2(0, g, bank_a[g], 0)
-            product(g, bank_a[g], 0, w3q, xq[0])
+        products(groups, bank_a, 0, w3q, xq[0])
         for g in groups:
             tanh_z1(0, g, bank_b[g], 0)
         interleave(vcopy, dyq[0])
         interleave(vcopy, woq)
         quantize(dyq[0])
         quantize(woq)
-        for g in groups:
-            product(g, bank_b[g], 0, woq, dyq[0])
+        products(groups, bank_b, 0, woq, dyq[0])
         v_diff(0, pairs[0])
         for g in lo:
             tanh_z3(0, g, bank_a[g], 0)
@@ -173,20 +171,18 @@ def tile_rows_bmixture_kernel(tc, x, w1, w2, w3, b3, wo, dy, old, out):
         for g in lo:
             v_dgt(0, g)
         quantize(xq[1])
-        for g in groups:
-            product(g, bank_a[g], 0, w2q, xq[1])
-            product(g, bank_a[g], HALF, w1q, xq[1])
+        products(groups, bank_a, 0, w2q, xq[1])
+        products(groups, bank_a, HALF, w1q, xq[1])
         interleave(scopy, dyq[1], slice(0, HALF))
         square(0, pairs[1])
         v_dz3(0, pairs[0])
         for g in hi:
             v_dgt(0, g)
+        quantize(dyq[1])
+        products(groups, bank_b, HALF, w3q, xq[1])
+        products(groups, bank_b, 0, woq, dyq[1])
         v_res(0, pairs[0])
         store(0, pairs[0])
-        quantize(dyq[1])
-        for g in groups:
-            product(g, bank_b[g], 0, woq, dyq[1])
-            product(g, bank_b[g], HALF, w3q, xq[1])
         for g in hi:
             v_dz3(0, one[g])
         for g in hi:

from contextlib import ExitStack

import concourse.mybir as mybir

G, D, M, N = 4, 128, 128, 512
FLOPS = 4 * 2 * G * D * M * N

F32 = mybir.dt.float32
BF16 = mybir.dt.bfloat16
U32 = mybir.dt.uint32
U8 = mybir.dt.uint8
FP8X4 = mybir.dt.float8_e4m3fn_x4
ACT = mybir.ActivationFunctionType
ALU = mybir.AluOpType

P = 128
PACK = 4
ROWS = D // PACK
HALF = N // 2
MM_N = 128
RUN = 4


def tile_rows_bmixture_kernel(tc, x, w1, w2, w3, b3, wo, dy, old, out):
    nc = tc.nc
    with ExitStack() as ctx:
        sb = ctx.enter_context(tc.tile_pool(name="sb", bufs=1))
        ps = ctx.enter_context(tc.psum_pool(name="ps", bufs=1))
        ctx.enter_context(tc.manual_schedule())

        def operand(name, width):
            return {
                "raw": sb.tile([P, PACK, width], F32, name=name + "_raw"),
                "bf": sb.tile([P, width, PACK], BF16, name=name + "_bf", align_bytes=64),
                "codes": sb.tile([P, width], U32, name=name + "_codes", align_bytes=64),
                "scales": sb.tile([P, width], U8, name=name + "_scales", align_bytes=64),
            }

        def load(op, src, cols):
            nc.sync.dma_start(out=op["raw"][:], in_=src.rearrange("g (p j) n -> (g p) j n", j=PACK)[:, :, cols])

        def interleave(copy, op, cols=slice(None)):
            copy(
                out=op["bf"][:, cols, :].rearrange("p (c i) j -> p c j i", i=RUN),
                in_=op["raw"][:, :, cols].rearrange("p j (c i) -> p c j i", i=RUN),
            )

        def quantize(op):
            nc.vector.quantize_mx(
                out=op["codes"][:].bitcast(FP8X4),
                scales=op["scales"][:],
                in_=op["bf"][:].rearrange("p n j -> p (n j)"),
            )

        def products(gs, banks, at, w, a):
            for n0 in range(0, HALF, MM_N):
                for g in gs:
                    rows = slice(ROWS * g, ROWS * (g + 1))
                    nc.tensor.matmul_mx(
                        out=banks[g][:, at + n0 : at + n0 + MM_N],
                        lhsT=w["codes"][rows, :].bitcast(FP8X4),
                        lhsT_scale=w["scales"][rows, :],
                        rhs=a["codes"][rows, n0 : n0 + MM_N].bitcast(FP8X4),
                        rhs_scale=a["scales"][rows, n0 : n0 + MM_N],
                        start=True,
                        stop=True,
                    )

        groups = range(G)
        halves = [slice(0, HALF), slice(HALF, N)]
        w1q, w2q, w3q, woq = operand("w1", M), operand("w2", M), operand("w3", M), operand("wo", M)
        xq = [operand("x0", HALF), operand("x1", HALF)]
        dyq = [operand("dy0", HALF), operand("dy1", HALF)]
        bank_a = [ps.tile([P, N], F32, name="bank_a%d" % g) for g in groups]
        bank_b = [ps.tile([P, N], F32, name="bank_b%d" % g) for g in groups]

        def half_tiles(name):
            return [sb.tile([P, G, HALF], F32, name="%s%d" % (name, h)) for h in range(2)]

        e1, e2, th, sq = half_tiles("e1"), half_tiles("e2"), half_tiles("th"), half_tiles("sq")
        diff, dgt, dz3, old_sb, res = half_tiles("diff"), half_tiles("dgt"), half_tiles("dz3"), half_tiles("old"), half_tiles("res")
        b_rows = sb.tile([P, G * ROWS], F32, align_bytes=64)
        b_cols = sb.tile([P, G * ROWS], F32, align_bytes=64)
        b_half = sb.tile([P, G], F32)

        def silu_z2(h, g, bank, at):
            nc.scalar.activation(out=e2[h][:, g, :], in_=bank[:, at : at + HALF], func=ACT.Silu)

        def tanh_z1(h, g, bank, at):
            nc.scalar.activation(out=e1[h][:, g, :], in_=bank[:, at : at + HALF], func=ACT.Tanh)

        def tanh_z3(h, g, bank, at):
            nc.scalar.activation(out=th[h][:, g, :], in_=bank[:, at : at + HALF], func=ACT.Tanh, bias=b_half[:, g : g + 1], scale=0.5)

        def square(h, gs):
            nc.scalar.activation(out=sq[h][:, gs, :], in_=th[h][:, gs, :], func=ACT.Square, scale=0.5)

        def v_diff(h, gs):
            nc.vector.tensor_tensor(out=diff[h][:, gs, :], in0=e2[h][:, gs, :], in1=e1[h][:, gs, :], op=ALU.subtract)

        def v_dgt(h, g):
            nc.vector.tensor_tensor(out=dgt[h][:, g, :], in0=bank_b[g][:, 0:HALF], in1=diff[h][:, g, :], op=ALU.mult)

        def v_dz3(h, gs):
            nc.vector.scalar_tensor_tensor(out=dz3[h][:, gs, :], in0=sq[h][:, gs, :], scalar=0.25, in1=dgt[h][:, gs, :], op0=ALU.subtract, op1=ALU.mult)

        def v_res(h, gs, engine=nc.vector):
            engine.tensor_tensor(out=res[h][:, gs, :], in0=dz3[h][:, gs, :], in1=old_sb[h][:, gs, :], op=ALU.add)

        def store(h, gs):
            nc.sync.dma_start(out=out.rearrange("g m n -> m g n")[:, gs, halves[h]], in_=res[h][:, gs, :])

        everything = slice(0, G)
        one = [slice(g, g + 1) for g in groups]
        pairs = [slice(0, 2), slice(2, 4)]

        warm_in = sb.tile([P, 1], F32)
        warm_out = sb.tile([P, 1], F32)
        nc.vector.memset(warm_in[:], 0.0)
        nc.vector.memset(b_rows[:], 0.0)
        nc.scalar.activation(out=warm_out[:], in_=warm_in[:], func=ACT.Silu)
        load(xq[0], x, halves[0])
        load(w2q, w2, slice(0, M))
        load(w1q, w1, slice(0, M))
        load(w3q, w3, slice(0, M))
        nc.sync.dma_start(
            out=b_rows[0:P:ROWS, :].rearrange("q (g i) -> q g i", g=G),
            in_=b3.rearrange("g (q i) o -> q g (i o)", i=ROWS),
        )
        load(dyq[0], dy, halves[0])
        load(woq, wo, slice(0, M))
        load(xq[1], x, halves[1])
        load(dyq[1], dy, halves[1])
        for h in range(2):
            nc.sync.dma_start(out=old_sb[h][:], in_=old.rearrange("g m n -> m g n")[:, :, halves[h]])

        vcopy, scopy = nc.vector.tensor_copy, nc.scalar.copy
        lo, hi = [0, 1], [2, 3]
        interleave(vcopy, xq[0], slice(0, 160))
        interleave(scopy, xq[0], slice(160, HALF))
        interleave(vcopy, w2q)
        quantize(xq[0])
        interleave(scopy, w1q)
        quantize(w2q)
        products(groups, bank_a, 0, w2q, xq[0])
        interleave(vcopy, w3q)
        quantize(w1q)
        products(groups, bank_b, 0, w1q, xq[0])
        nc.vector.transpose(out=b_cols[:], in_=b_rows[:])
        quantize(w3q)
        nc.vector.tensor_scalar(out=b_half[:], in0=b_cols[:, 0 : G * ROWS : ROWS], scalar1=0.5, scalar2=None, op0=ALU.mult)
        for g in groups:
            silu_z2(0, g, bank_a[g], 0)
        products(groups, bank_a, 0, w3q, xq[0])
        for g in groups:
            tanh_z1(0, g, bank_b[g], 0)
        interleave(vcopy, dyq[0])
        interleave(vcopy, woq)
        quantize(dyq[0])
        quantize(woq)
        products(groups, bank_b, 0, woq, dyq[0])
        v_diff(0, pairs[0])
        for g in lo:
            tanh_z3(0, g, bank_a[g], 0)
        interleave(scopy, xq[1], slice(192, HALF))
        tanh_z3(0, 2, bank_a[2], 0)
        square(0, pairs[0])
        tanh_z3(0, 3, bank_a[3], 0)
        interleave(vcopy, xq[1], slice(0, 192))
        v_diff(0, pairs[1])
        for g in lo:
            v_dgt(0, g)
        quantize(xq[1])
        products(groups, bank_a, 0, w2q, xq[1])
        products(groups, bank_a, HALF, w1q, xq[1])
        interleave(scopy, dyq[1], slice(0, HALF))
        square(0, pairs[1])
        v_dz3(0, pairs[0])
        for g in hi:
            v_dgt(0, g)
        quantize(dyq[1])
        products(groups, bank_b, HALF, w3q, xq[1])
        products(groups, bank_b, 0, woq, dyq[1])
        v_res(0, pairs[0])
        store(0, pairs[0])
        for g in hi:
            v_dz3(0, one[g])
        for g in hi:
            v_res(0, one[g])
        store(0, pairs[1])
        for pair in (lo, hi):
            for g in pair:
                silu_z2(1, g, bank_a[g], 0)
                tanh_z1(1, g, bank_a[g], HALF)
            for g in pair:
                tanh_z3(1, g, bank_b[g], HALF)
            for g in pair:
                square(1, one[g])
            for step in (v_diff, v_dgt, v_dz3):
                for g in pair:
                    step(1, g if step == v_dgt else one[g])
            for g in pair:
                v_res(1, one[g])
                store(1, one[g])
